import numpy as np
import ml_dtypes


def mxq(x, axis, fmt="e4m3"):
    dtype, down = {"e4m3": (ml_dtypes.float8_e4m3fn, 7), "e5m2": (ml_dtypes.float8_e5m2, 14)}[fmt]
    v = np.moveaxis(np.asarray(x, np.float32).astype(ml_dtypes.bfloat16).astype(np.float64), axis, -1)
    blocks = v.reshape(v.shape[:-1] + (-1, 32))
    amax = np.abs(blocks).max(-1, keepdims=True)
    byte = np.maximum(np.where(amax > 0, np.frexp(amax)[1] - 1 + 127, 0) - down, 1)
    scale = np.exp2(byte - 127.0)
    codes = (blocks / scale).astype(np.float32).astype(dtype).astype(np.float64)
    return np.moveaxis((codes * scale).reshape(v.shape), -1, axis)


WIDE = False


def mx_kscale(k):
    if not WIDE:
        return np.ones(k)
    levels = np.array([10, -10, 5, -5, 0])
    if k % 512:
        return np.exp2(np.random.permutation(np.resize(levels, k // 32))).repeat(32)
    a = np.empty((k // 512, 16))
    for p in range(k // 512):
        a[p, :8] = np.random.permutation(np.resize(levels, 8))
        for g in range(8):
            far = levels[np.abs(levels - a[p, g]) >= 10]
            a[p, g + 8] = far[np.random.randint(len(far))]
    return np.exp2(a.ravel()).repeat(32)


def f64(x):
    return np.asarray(x).astype(np.float64)


def striped(idx):
    return np.tile(idx.reshape(-1, 16).T, (8, 1)).astype(np.uint16)


def unstriped(offs):
    return offs[:16].T.reshape(-1).astype(np.int64)


def striped8(idx):
    return np.concatenate([x.reshape(-1, 16).T for x in idx]).astype(np.uint16)


def runs(offs, k):
    lists = np.stack([offs[16 * r : 16 * r + 16].T.reshape(-1) for r in range(8)]).astype(np.int64)
    return lists[np.arange(k) % 512 // 64]


def pack_weight(w):
    k, n = w.shape
    w = f64(np.asarray(w, np.float32).astype(ml_dtypes.bfloat16)).reshape(k // 32, 32, n)
    amax = np.abs(w).max(1)
    byte = np.clip(np.where(amax > 0, np.frexp(amax)[1] - 1 + 127 - 7, 1), 1, 254)
    scaled = (w * np.exp2(127.0 - byte)[:, None, :]).reshape(k, n).astype(np.float32)
    words = np.ascontiguousarray(scaled.reshape(k // 512, 128, 4, n).transpose(0, 1, 3, 2)).astype(ml_dtypes.float8_e4m3fn).view(np.uint8)
    return words, np.ascontiguousarray(byte.astype(np.uint8).reshape(k // 512, 16, n))


def unpack_weight(words, scales):
    g, p, n, _ = words.shape
    vals = np.ascontiguousarray(words).view(ml_dtypes.float8_e4m3fn).astype(np.float64) * np.repeat(np.exp2(scales.astype(np.float64) - 127.0), 8, axis=1)[..., None]
    return vals.transpose(0, 1, 3, 2).reshape(g * 512, n)


E2M1 = np.array([0.0, 0.5, 1.0, 1.5, 2.0, 3.0, 4.0, 6.0, -0.0, -0.5, -1.0, -1.5, -2.0, -3.0, -4.0, -6.0])


def pack_fp4(w):
    k, n = w.shape
    w = f64(np.asarray(w, np.float32).astype(ml_dtypes.bfloat16)).reshape(k // 32, 32, n)
    amax = np.abs(w).max(1)
    mant, ex = np.frexp(amax / 6.0)
    byte = np.clip(np.where(amax > 0, np.where(mant > 0.5, ex, ex - 1) + 127, 1), 1, 254)
    scaled = (w * np.exp2(127.0 - byte)[:, None, :]).reshape(k, n).astype(np.float32)
    c = np.ascontiguousarray(scaled.reshape(k // 512, 128, 4, n).transpose(0, 1, 3, 2)).astype(ml_dtypes.float4_e2m1fn).view(np.uint8) & 0xF
    words = (c[..., 0::2] | (c[..., 1::2] << 4)).reshape(k // 512, 128, 2 * n)
    return np.ascontiguousarray(words), np.ascontiguousarray(byte.astype(np.uint8).reshape(k // 512, 16, n))


def unpack_fp4(words, scales):
    g, _, n = scales.shape
    words = np.ascontiguousarray(words).reshape(g, 128, n, 2)
    nib = np.empty((g, 128, n, 4), np.uint8)
    nib[..., 0::2] = words & 0xF
    nib[..., 1::2] = words >> 4
    vals = E2M1[nib] * np.repeat(np.exp2(scales.astype(np.float64) - 127.0), 8, axis=1)[..., None]
    return vals.transpose(0, 1, 3, 2).reshape(g * 512, n)


def relu(v):
    return np.maximum(v, 0.0)

def planes(y):
    n, m = y.shape
    v = y.astype(np.float32).astype(ml_dtypes.bfloat16).astype(np.float64).reshape(n // 32, 32, m)
    top = np.abs(v).max(1)
    byte = np.clip(np.where(top > 0, np.frexp(top)[1] - 1 + 127 - 7, 1), 1, 254)
    codes = (v * np.exp2(127.0 - byte)[:, None, :]).reshape(n, m).astype(np.float32).astype(ml_dtypes.float8_e4m3fn).view(np.uint8)
    words = codes.reshape(n // 512, 128, 4, m).transpose(0, 1, 3, 2)
    return np.ascontiguousarray(words), np.ascontiguousarray(byte.astype(np.uint8).reshape(n // 512, 16, m))


K, T, S, N, H = 512, 2048, 512, 512, 512


def setup_inputs():
    n = np.random.standard_normal
    s = mx_kscale(K)[:, None]
    u = mx_kscale(S)
    packed_xT = pack_weight(n((K, T)) * s)
    packed_w1 = pack_fp4(n((S, H)) / np.sqrt(S) / u[:, None])
    packed_w2 = pack_fp4(n((H, N)) / np.sqrt(H) / u[:, None])
    return {
        "x_words": packed_xT[0],
        "x_scales": packed_xT[1],
        "wa": (n((K, H)) / np.sqrt(K) / s).astype(np.float32),
        "gt": (np.random.uniform(0.5, 1.5, (S, 1)) * u[:, None]).astype(np.float32),
        "w1_words": packed_w1[0],
        "w1_scales": packed_w1[1],
        "gp": (np.random.uniform(0.5, 1.5, (H, 1)) * u[:, None]).astype(np.float32),
        "res": (1.5 * n((N, H))).astype(np.float32),
        "w2_words": packed_w2[0],
        "w2_scales": packed_w2[1],
        "offs": striped(np.random.permutation(T)[:S]),
        "fl": striped8(np.stack([np.random.permutation(H) for _ in range(8)])),
        "fm": striped8(np.stack([np.random.permutation(H) for _ in range(8)])),
    }


def reference(x_words, x_scales, wa, gt, w1_words, w1_scales, gp, res, w2_words, w2_scales, offs, fl, fm):
    xq = unpack_weight(x_words, x_scales)[:, unstriped(offs)]
    y = xq.T @ mxq(f64(wa), 0, "e4m3")
    z = f64(gt) * (y[np.arange(S)[:, None], runs(fl, S)])
    h = relu(unpack_fp4(w1_words, w1_scales).T @ mxq(z, 0, "e4m3"))
    z2 = f64(gp) * (h[np.arange(H)[:, None], runs(fm, H)])
    out_0 = f64(res) + (unpack_fp4(w2_words, w2_scales).T @ mxq(z2, 0, "e4m3"))
    return (out_0,) + planes(out_0)

@@ -1,0 +1,252 @@
+from contextlib import ExitStack
+
+import concourse.mybir as mybir
+
+F32 = mybir.dt.float32
+BF16 = mybir.dt.bfloat16
+I32 = mybir.dt.int32
+U32 = mybir.dt.uint32
+U16 = mybir.dt.uint16
+U8 = mybir.dt.uint8
+FP8X4 = mybir.dt.float8_e4m3fn_x4
+FP4X4 = mybir.dt.float4_e2m1fn_x4
+ACT = mybir.ActivationFunctionType
+ALU = mybir.AluOpType
+
+P = 128
+PACK = 4
+D = 512
+T = 2048
+QUADS = 4
+FLOPS = 3 * 2 * D * D * D
+
+WA_CHUNKS = ((0, 128), (128, 128), (256, 128), (384, 128))
+WA_QUANT = ((0, 256), (256, 128), (384, 128))
+Z_CHUNKS = ((0, 256), (256, 128), (384, 128))
+OUT_CHUNKS = ((0, 128), (128, 128), (256, 128), (384, 128))
+
+
+def tile_picked_mixdeep_relu_po_kernel(
+    tc, x_words, x_scales, wa, gt, w1_words, w1_scales, gp, res, w2_words, w2_scales, offs, fl, fm, out_0, out_1, out_2
+):
+    nc = tc.nc
+    with ExitStack() as ctx:
+        lists = ctx.enter_context(tc.tile_pool(name="lists", bufs=1))
+        keep = ctx.enter_context(tc.tile_pool(name="keep", bufs=1))
+        psum = ctx.enter_context(tc.psum_pool(name="psum", bufs=1))
+
+        def sb(shape, dtype, name, tag=None):
+            return keep.tile(shape, dtype, name=name, tag=tag or name, align_bytes=64)
+
+        def load_scale_rows(queue, tile, scales):
+            for q in range(QUADS):
+                queue.dma_start(out=tile[32 * q : 32 * q + 4, :].bitcast(I32), in_=scales[0, 4 * q : 4 * q + 4, :].bitcast(I32))
+
+        def weave(engine, planes, name, as_activation=False, tag=None):
+            woven = sb([P, planes.shape[2], PACK], BF16, name, tag)
+            weave_into(engine, planes, woven[:], as_activation)
+            return woven[:]
+
+        def weave_into(engine, planes, woven, as_activation=False):
+            dst = woven.rearrange("p (c i) t -> p c t i", i=4)
+            src = planes.rearrange("p t (c i) -> p c t i", i=4)
+            if as_activation:
+                nc.scalar.activation(out=dst, in_=src, func=ACT.Copy)
+            elif engine == "scalar":
+                nc.scalar.copy(out=dst, in_=src)
+            else:
+                nc.vector.tensor_copy(out=dst, in_=src)
+
+        def quantize(woven, codes, scales):
+            nc.vector.quantize_mx(out=codes.bitcast(FP8X4), scales=scales, in_=woven.rearrange("p n t -> p (n t)"))
+
+        def deal_words(pieces, name, tag=None):
+            dealt = sb([P, 2 * D], U8, name, tag)
+            m = P // len(pieces)
+            for i, words in enumerate(pieces):
+                nc.vector.tensor_copy(
+                    out=dealt[:].rearrange("p (t m b) -> p m t b", t=PACK, b=2)[:, i * m : (i + 1) * m, :, :],
+                    in_=words[:].rearrange("p (m t b) -> p m t b", t=PACK, b=2),
+                )
+            return dealt
+
+        def deal_scales(scales, name, tag=None):
+            dealt = sb([P, D], U8, name, tag)
+            nc.vector.tensor_copy(
+                out=dealt[:].rearrange("p (t m) -> p m t", t=PACK),
+                in_=scales.rearrange("p (m t) -> p m t", t=PACK),
+            )
+            return dealt
+
+        offs_t = lists.tile([P, D // 16], U16, name="offs_t")
+        fl_t = lists.tile([P, D // 16], U16, name="fl_t")
+        fm_t = lists.tile([P, D // 16], U16, name="fm_t")
+        xs = sb([P, T], U8, "xs")
+        xw = sb([P, T], U32, "xw")
+        w1w = [sb([P, D], U8, "w1w%d" % h) for h in range(2)]
+        gt_t = sb([P, PACK], F32, "gt_t")
+        gp_t = sb([P, PACK], F32, "gp_t")
+
+        nc.vector.memset(xs[:].bitcast(I32), 0)
+
+        for h in range(2):
+            nc.sync.dma_start(out=w1w[h][:].bitcast(I32), in_=w1_words[0][:, h * D : (h + 1) * D].bitcast(I32))
+        nc.sync.dma_start(offs_t[:], offs)
+        nc.sync.dma_start(fl_t[:], fl)
+        nc.sync.dma_start(out=xw[:].bitcast(I32), in_=x_words[0].rearrange("p n t -> p (n t)").bitcast(I32))
+        nc.sync.dma_start(fm_t[:], fm)
+        load_scale_rows(nc.sync, xs[:], x_scales)
+        nc.gpsimd.dma_start(out=gt_t[:], in_=gt.rearrange("(p t) o -> p (t o)", t=PACK))
+        nc.gpsimd.dma_start(out=gp_t[:], in_=gp.rearrange("(p t) o -> p (t o)", t=PACK))
+
+        w1d = deal_words(w1w, "w1d")
+
+        wa_rows = wa.rearrange("(p t) n -> p t n", t=PACK)
+        wa_half = [sb([P, PACK * D // 2], F32, "wa_half%d" % h, "w1w%d" % h) for h in range(2)]
+        wa_raw = []
+        for c0, n in WA_CHUNKS:
+            h, c = divmod(c0, D // 2)
+            raw = wa_half[h][:, PACK * c : PACK * (c + n)].rearrange("p (t n) -> p t n", t=PACK)
+            nc.sync.dma_start(out=raw, in_=wa_rows[:, :, c0 : c0 + n])
+            wa_raw.append(raw)
+
+        xs_picked = sb([P, D], U8, "xs_picked")
+        xs_dealt = sb([P, D], U8, "xs_dealt")
+        xw_dealt = sb([P, D], U32, "xw_dealt")
+        nc.vector.tensor_copy(out=xs_picked[:], in_=xs[:].indirect(offs_t[:]))
+        nc.vector.tensor_copy(out=xw_dealt[:].rearrange("p (t m) -> p m t", t=PACK), in_=xw[:].indirect(offs_t[:]))
+        nc.vector.tensor_copy(
+            out=xs_dealt[:].rearrange("p (t m) -> p m t", t=PACK),
+            in_=xs_picked[:].rearrange("p (m t) -> p m t", t=PACK),
+        )
+
+        ws = sb([P, 2 * D], U8, "ws", "xw")
+        nc.gpsimd.memset(ws[:].bitcast(I32), 0)
+        w1s = ws[:, 0:D]
+        w2s = ws[:, D : 2 * D]
+        load_scale_rows(nc.sync, w1s, w1_scales)
+        load_scale_rows(nc.sync, w2s, w2_scales)
+        w2w = sb([P, 2 * D], U8, "w2w", "xs_picked")
+        nc.sync.dma_start(out=w2w[:].bitcast(I32), in_=w2_words[0].bitcast(I32))
+        res_t = sb([P, PACK, D], F32, "res_t", "xs")
+        nc.sync.dma_start(out=res_t[:], in_=res.rearrange("(p t) n -> p t n", t=PACK))
+
+        y_banks = [psum.tile([P, D], F32, name="y_bank%d" % t, tag="bank%d" % t) for t in range(PACK)]
+        wa_woven = [sb([P, n, PACK], BF16, "wa_woven%d" % i) for i, (c0, n) in enumerate(WA_QUANT)]
+        weave_into("scalar", wa_raw[0], wa_woven[0][:, 0:128, :], True)
+        weave_into("scalar", wa_raw[1], wa_woven[0][:, 128:256, :])
+        weave_into("scalar", wa_raw[2], wa_woven[1][:])
+        weave_into("vector", wa_raw[3], wa_woven[2][:])
+        wa_codes = sb([P, D], U32, "wa_codes")
+        wa_scales = sb([P, D], U8, "wa_scales")
+        for i, (c0, n) in enumerate(WA_QUANT):
+            cols = slice(c0, c0 + n)
+            quantize(wa_woven[i][:], wa_codes[:, cols], wa_scales[:, cols])
+        for t in range(PACK):
+            for c0, n in WA_QUANT if t == 0 else ((0, D),):
+                cols = slice(c0, c0 + n)
+                m = slice(t * P, (t + 1) * P)
+                nc.tensor.matmul_mx(
+                    out=y_banks[t][:, cols], lhsT=xw_dealt[:, m].bitcast(FP8X4), lhsT_scale=xs_dealt[:, m],
+                    rhs=wa_codes[:, cols].bitcast(FP8X4), rhs_scale=wa_scales[:, cols], start=True, stop=True,
+                )
+        y_rows = [sb([P, D], F32, "y_rows%d" % t) for t in range(PACK)]
+        for t in range(PACK):
+            nc.scalar.activation(out=y_rows[t][:], in_=y_banks[t][:], func=ACT.Copy, scale=gt_t[:, t : t + 1])
+
+        w1sd = deal_scales(w1s, "w1sd", "wa_woven1")
+        w2sd = deal_scales(w2s, "w2sd", "wa_woven2")
+
+        def mix(codes, scales, n, words, wscales, first_bank, per_bank, name):
+            views = []
+            banks = []
+            for b in range(PACK // per_bank):
+                bank = psum.tile([P, per_bank, n], F32, name="%s_%d" % (name, b), tag="bank%d" % (first_bank + b))
+                banks.append(bank)
+                for u in range(per_bank):
+                    t = b * per_bank + u
+                    nc.tensor.matmul_mx(
+                        out=bank[:, u, :], lhsT=words[:, 2 * P * t : 2 * P * (t + 1)].bitcast(FP4X4),
+                        lhsT_scale=wscales[:, P * t : P * (t + 1)],
+                        rhs=codes.bitcast(FP8X4), rhs_scale=scales, start=True, stop=True,
+                    )
+                    views.append(bank[:, u, :])
+            return banks, views
+
+        h_rows = [sb([P, D], F32, "h_rows%d" % t) for t in range(PACK)]
+        z_space = sb([P, PACK * D], BF16, "z_space")
+        z_codes = sb([P, D], U32, "z_codes")
+        z_scales = sb([P, D], U8, "z_scales")
+        for i, (c0, n) in enumerate(Z_CHUNKS):
+            cols = slice(c0, c0 + n)
+            if i < 2:
+                z_planes = sb([P, PACK, n], BF16, "z_planes%d" % i)[:]
+            else:
+                z_planes = z_space[:].rearrange("p (t n) -> p t n", t=PACK)[:, :, 0:n]
+            for t in range(PACK):
+                nc.vector.tensor_copy(out=z_planes[:, t, :], in_=y_rows[t][:].indirect(fl_t[:, c0 // 16 : (c0 + n) // 16]))
+            if i < 2:
+                woven = z_space[:, D + PACK * c0 : D + PACK * (c0 + n)].rearrange("p (n t) -> p n t", t=PACK)
+                weave_into("scalar", z_planes, woven)
+            else:
+                woven = weave("vector", z_planes, "z_woven%d" % i)
+            quantize(woven, z_codes[:, cols], z_scales[:, cols])
+            banks, views = mix(z_codes[:, cols], z_scales[:, cols], n, w1d, w1sd, (4, 6, 0)[i], (2, 4, 1)[i], "h_bank%d" % i)
+            for t in range(PACK):
+                nc.scalar.activation(out=h_rows[t][:, cols], in_=views[t], func=ACT.Relu)
+
+        w2d = deal_words([w2w], "w2d", "z_woven2")
+
+        z2_codes = sb([P, D], U32, "z2_codes")
+        z2_scales = sb([P, D], U8, "z2_scales")
+        o_codes = sb([P, D], U32, "o_codes")
+        o_scales = sb([P, D], U8, "o_scales")
+        out_rows = out_0.rearrange("(p t) n -> p t n", t=PACK)
+        out_words = out_1[0].rearrange("p n t -> p (n t)").bitcast(I32)
+        o_banks = []
+        h_space = [sb([P, D], F32, "h_space%d" % i) for i in range(2)]
+        for i, (c0, n) in enumerate(OUT_CHUNKS):
+            cols = slice(c0, c0 + n)
+            if i < 2:
+                h_planes = sb([P, PACK, n], F32, "h_planes%d" % i)[:]
+            else:
+                h_planes = h_space[i - 2][:].rearrange("p (t n) -> p t n", t=PACK)
+            z2_planes = sb([P, PACK, n], BF16, "z2_planes%d" % i)
+            for t in range(PACK):
+                nc.vector.tensor_copy(out=h_planes[:, t, :], in_=h_rows[t][:].indirect(fm_t[:, c0 // 16 : (c0 + n) // 16]))
+                nc.scalar.activation(out=z2_planes[:, t, :], in_=h_planes[:, t, :], func=ACT.Copy, scale=gp_t[:, t : t + 1])
+            if i < 2:
+                woven = h_space[i][:, n : 3 * n].bitcast(BF16).rearrange("p (n t) -> p n t", t=PACK)
+                weave_into("scalar", z2_planes[:], woven)
+            else:
+                woven = weave("scalar", z2_planes[:], "z2_woven%d" % i, tag="ring%d" % (i % 2))
+            quantize(woven, z2_codes[:, cols], z2_scales[:, cols])
+            banks, views = mix(z2_codes[:, cols], z2_scales[:, cols], n, w2d, w2sd, (7, 4, 5, 6)[i], PACK, "o_bank%d" % i)
+            o_banks.append(banks[0])
+
+        def finish(i, tag, parts, store_from):
+            c0, n = OUT_CHUNKS[i]
+            o_planes = sb([P, PACK, n], F32, "o_planes%d" % i, tag)
+            o_woven = sb([P, n, PACK], BF16, "o_woven%d" % i)
+            w = n // parts
+            for j in range(parts):
+                part = slice(j * w, (j + 1) * w)
+                cols = slice(c0 + j * w, c0 + (j + 1) * w)
+                nc.vector.tensor_tensor(out=o_planes[:, :, part], in0=o_banks[i][:, :, part], in1=res_t[:, :, cols], op=ALU.add)
+            nc.sync.dma_start(out=out_rows[:, :, c0 : c0 + n], in_=o_planes[:])
+            for j in range(parts):
+                part = slice(j * w, (j + 1) * w)
+                cols = slice(c0 + j * w, c0 + (j + 1) * w)
+                weave_into("scalar", o_planes[:, :, part], o_woven[:, part, :])
+                quantize(o_woven[:, part, :], o_codes[:, cols], o_scales[:, cols])
+            if store_from is not None:
+                cols = slice(store_from[0], store_from[1])
+                nc.sync.dma_start(out=out_words[:, cols], in_=o_codes[:, cols].bitcast(I32))
+
+        finish(1, None, 1, None)
+        finish(0, "ring0", 1, (0, 256))
+        finish(2, "ring1", 1, (256, 384))
+        finish(3, None, 2, (384, 512))
+        for q in range(QUADS):
+            queue = nc.sync if q % 2 == 0 else nc.scalar
+            queue.dma_start(out=out_2[0, 4 * q : 4 * q + 4, :].bitcast(I32), in_=o_scales[32 * q : 32 * q + 4, :].bitcast(I32))

@@ -38,9 +38,12 @@ def tile_picked_mixdeep_relu_po_kernel(
         def sb(shape, dtype, name, tag=None):
             return keep.tile(shape, dtype, name=name, tag=tag or name, align_bytes=64)
 
-        def load_scale_rows(queue, tile, scales):
+        def place_scale_rows(plane, staged, first):
             for q in range(QUADS):
-                queue.dma_start(out=tile[32 * q : 32 * q + 4, :].bitcast(I32), in_=scales[0, 4 * q : 4 * q + 4, :].bitcast(I32))
+                nc.sync.dma_start(
+                    out=plane[32 * q : 32 * q + 4, :].bitcast(I32),
+                    in_=staged[first + 4 * q : first + 4 * q + 4, :].bitcast(I32),
+                )
 
         def weave(engine, planes, name, as_activation=False, tag=None):
             woven = sb([P, planes.shape[2], PACK], BF16, name, tag)
@@ -60,21 +63,11 @@ def tile_picked_mixdeep_relu_po_kernel(
         def quantize(woven, codes, scales):
             nc.vector.quantize_mx(out=codes.bitcast(FP8X4), scales=scales, in_=woven.rearrange("p n t -> p (n t)"))
 
-        def deal_words(pieces, name, tag=None):
-            dealt = sb([P, 2 * D], U8, name, tag)
-            m = P // len(pieces)
-            for i, words in enumerate(pieces):
-                nc.vector.tensor_copy(
-                    out=dealt[:].rearrange("p (t m b) -> p m t b", t=PACK, b=2)[:, i * m : (i + 1) * m, :, :],
-                    in_=words[:].rearrange("p (m t b) -> p m t b", t=PACK, b=2),
-                )
-            return dealt
-
-        def deal_scales(scales, name, tag=None):
-            dealt = sb([P, D], U8, name, tag)
+        def deal(words, name, dtype, width, tag=None):
+            dealt = sb([P, width * D], dtype, name, tag)
             nc.vector.tensor_copy(
-                out=dealt[:].rearrange("p (t m) -> p m t", t=PACK),
-                in_=scales.rearrange("p (m t) -> p m t", t=PACK),
+                out=dealt[:].rearrange("p (t m b) -> p t m b", t=PACK, b=width),
+                in_=words[:].rearrange("p (m t b) -> p t m b", t=PACK, b=width),
             )
             return dealt
 
@@ -83,52 +76,50 @@ def tile_picked_mixdeep_relu_po_kernel(
         fm_t = lists.tile([P, D // 16], U16, name="fm_t")
         xs = sb([P, T], U8, "xs")
         xw = sb([P, T], U32, "xw")
-        w1w = [sb([P, D], U8, "w1w%d" % h) for h in range(2)]
-        gt_t = sb([P, PACK], F32, "gt_t")
-        gp_t = sb([P, PACK], F32, "gp_t")
+        ws = sb([P, D], U8, "ws")
+        xs_plane = sb([P, D], U8, "xs_plane")
+        ws_planes = sb([P, 2 * D], U8, "ws_planes")
 
-        nc.vector.memset(xs[:].bitcast(I32), 0)
+        nc.vector.memset(xs[0:112, :].bitcast(I32), 0)
+        nc.vector.memset(ws[0:96, :].bitcast(I32), 0)
+        nc.vector.memset(xs_plane[:].bitcast(I32), 0)
+        nc.vector.memset(ws_planes[:].bitcast(I32), 0)
 
-        for h in range(2):
-            nc.sync.dma_start(out=w1w[h][:].bitcast(I32), in_=w1_words[0][:, h * D : (h + 1) * D].bitcast(I32))
         nc.sync.dma_start(offs_t[:], offs)
-        nc.sync.dma_start(fl_t[:], fl)
+        nc.sync.dma_start(out=xs[112:128, :].bitcast(I32), in_=x_scales[0].bitcast(I32))
         nc.sync.dma_start(out=xw[:].bitcast(I32), in_=x_words[0].rearrange("p n t -> p (n t)").bitcast(I32))
+        nc.sync.dma_start(fl_t[:], fl)
         nc.sync.dma_start(fm_t[:], fm)
-        load_scale_rows(nc.sync, xs[:], x_scales)
-        nc.gpsimd.dma_start(out=gt_t[:], in_=gt.rearrange("(p t) o -> p (t o)", t=PACK))
-        nc.gpsimd.dma_start(out=gp_t[:], in_=gp.rearrange("(p t) o -> p (t o)", t=PACK))
-
-        w1d = deal_words(w1w, "w1d")
-
+        nc.gpsimd.dma_start(out=ws[96:112, :].bitcast(I32), in_=w1_scales[0].bitcast(I32))
+        nc.gpsimd.dma_start(out=ws[112:128, :].bitcast(I32), in_=w2_scales[0].bitcast(I32))
         wa_rows = wa.rearrange("(p t) n -> p t n", t=PACK)
-        wa_half = [sb([P, PACK * D // 2], F32, "wa_half%d" % h, "w1w%d" % h) for h in range(2)]
         wa_raw = []
         for c0, n in WA_CHUNKS:
-            h, c = divmod(c0, D // 2)
-            raw = wa_half[h][:, PACK * c : PACK * (c + n)].rearrange("p (t n) -> p t n", t=PACK)
-            nc.sync.dma_start(out=raw, in_=wa_rows[:, :, c0 : c0 + n])
-            wa_raw.append(raw)
+            raw = sb([P, PACK, n], F32, "wa_raw%d" % c0)
+            nc.sync.dma_start(out=raw[:], in_=wa_rows[:, :, c0 : c0 + n])
+            wa_raw.append(raw[:])
 
         xs_picked = sb([P, D], U8, "xs_picked")
-        xs_dealt = sb([P, D], U8, "xs_dealt")
-        xw_dealt = sb([P, D], U32, "xw_dealt")
         nc.vector.tensor_copy(out=xs_picked[:], in_=xs[:].indirect(offs_t[:]))
+        xs_staged = deal(xs_picked, "xs_staged", U8, 1)
+        place_scale_rows(xs_plane, xs_staged, 112)
+        xs_dealt = xs_plane
+        gt_t = sb([P, PACK], F32, "gt_t", "xs_picked")
+        nc.sync.dma_start(out=gt_t[:], in_=gt.rearrange("(p t) o -> p (t o)", t=PACK))
+        xw_dealt = sb([P, D], U32, "xw_dealt")
         nc.vector.tensor_copy(out=xw_dealt[:].rearrange("p (t m) -> p m t", t=PACK), in_=xw[:].indirect(offs_t[:]))
-        nc.vector.tensor_copy(
-            out=xs_dealt[:].rearrange("p (t m) -> p m t", t=PACK),
-            in_=xs_picked[:].rearrange("p (m t) -> p m t", t=PACK),
-        )
-
-        ws = sb([P, 2 * D], U8, "ws", "xw")
-        nc.gpsimd.memset(ws[:].bitcast(I32), 0)
-        w1s = ws[:, 0:D]
-        w2s = ws[:, D : 2 * D]
-        load_scale_rows(nc.sync, w1s, w1_scales)
-        load_scale_rows(nc.sync, w2s, w2_scales)
-        w2w = sb([P, 2 * D], U8, "w2w", "xs_picked")
+        ws_staged = deal(ws, "ws_staged", U8, 1, "xw")
+        w1w = sb([P, 2 * D], U8, "w1w", "wa_raw0")
+        nc.sync.dma_start(out=w1w[:].bitcast(I32), in_=w1_words[0].bitcast(I32))
+        w1sd = ws_planes[:, 0:D]
+        w2sd = ws_planes[:, D : 2 * D]
+        place_scale_rows(w1sd, ws_staged, 96)
+        place_scale_rows(w2sd, ws_staged, 112)
+        w2w = sb([P, 2 * D], U8, "w2w", "wa_raw128")
         nc.sync.dma_start(out=w2w[:].bitcast(I32), in_=w2_words[0].bitcast(I32))
-        res_t = sb([P, PACK, D], F32, "res_t", "xs")
+        gp_t = sb([P, PACK], F32, "gp_t", "wa_raw256")
+        nc.sync.dma_start(out=gp_t[:], in_=gp.rearrange("(p t) o -> p (t o)", t=PACK))
+        res_t = sb([P, PACK, D], F32, "res_t", "wa_raw384")
         nc.sync.dma_start(out=res_t[:], in_=res.rearrange("(p t) n -> p t n", t=PACK))
 
         y_banks = [psum.tile([P, D], F32, name="y_bank%d" % t, tag="bank%d" % t) for t in range(PACK)]
@@ -154,48 +145,46 @@ def tile_picked_mixdeep_relu_po_kernel(
         for t in range(PACK):
             nc.scalar.activation(out=y_rows[t][:], in_=y_banks[t][:], func=ACT.Copy, scale=gt_t[:, t : t + 1])
 
-        w1sd = deal_scales(w1s, "w1sd", "wa_woven1")
-        w2sd = deal_scales(w2s, "w2sd", "wa_woven2")
+        w1d = deal(w1w, "w1d", U8, 2, "wa_woven2")
 
-        def mix(codes, scales, n, words, wscales, first_bank, per_bank, name):
-            views = []
-            banks = []
-            for b in range(PACK // per_bank):
-                bank = psum.tile([P, per_bank, n], F32, name="%s_%d" % (name, b), tag="bank%d" % (first_bank + b))
-                banks.append(bank)
-                for u in range(per_bank):
-                    t = b * per_bank + u
-                    nc.tensor.matmul_mx(
-                        out=bank[:, u, :], lhsT=words[:, 2 * P * t : 2 * P * (t + 1)].bitcast(FP4X4),
-                        lhsT_scale=wscales[:, P * t : P * (t + 1)],
-                        rhs=codes.bitcast(FP8X4), rhs_scale=scales, start=True, stop=True,
-                    )
-                    views.append(bank[:, u, :])
-            return banks, views
+        def mix(outs, codes, scales, words, wscales):
+            for t in range(PACK):
+                nc.tensor.matmul_mx(
+                    out=outs[t], lhsT=words[:, 2 * P * t : 2 * P * (t + 1)].bitcast(FP4X4),
+                    lhsT_scale=wscales[:, P * t : P * (t + 1)],
+                    rhs=codes.bitcast(FP8X4), rhs_scale=scales, start=True, stop=True,
+                )
 
         h_rows = [sb([P, D], F32, "h_rows%d" % t) for t in range(PACK)]
-        z_space = sb([P, PACK * D], BF16, "z_space")
+        z_space = sb([P, 1920], BF16, "z_space")
         z_codes = sb([P, D], U32, "z_codes")
         z_scales = sb([P, D], U8, "z_scales")
+        first_banks = [psum.tile([P, 2, 256], F32, name="h_first%d" % b, tag="bank%d" % (4 + b)) for b in range(2)]
+        second_banks = [psum.tile([P, 256], F32, name="h_second%d" % t, tag="bank%d" % t) for t in range(PACK)]
         for i, (c0, n) in enumerate(Z_CHUNKS):
             cols = slice(c0, c0 + n)
             if i < 2:
                 z_planes = sb([P, PACK, n], BF16, "z_planes%d" % i)[:]
             else:
-                z_planes = z_space[:].rearrange("p (t n) -> p t n", t=PACK)[:, :, 0:n]
+                z_planes = z_space[:, 0:1536].rearrange("p (t n) -> p t n", t=PACK)[:, :, 0:n]
             for t in range(PACK):
                 nc.vector.tensor_copy(out=z_planes[:, t, :], in_=y_rows[t][:].indirect(fl_t[:, c0 // 16 : (c0 + n) // 16]))
-            if i < 2:
-                woven = z_space[:, D + PACK * c0 : D + PACK * (c0 + n)].rearrange("p (n t) -> p n t", t=PACK)
-                weave_into("scalar", z_planes, woven)
-            else:
-                woven = weave("vector", z_planes, "z_woven%d" % i)
+            at = 384 if i == 0 else 1408
+            woven = z_space[:, at : at + PACK * n].rearrange("p (n t) -> p n t", t=PACK)
+            weave_into("scalar" if i < 2 else "vector", z_planes, woven)
             quantize(woven, z_codes[:, cols], z_scales[:, cols])
-            banks, views = mix(z_codes[:, cols], z_scales[:, cols], n, w1d, w1sd, (4, 6, 0)[i], (2, 4, 1)[i], "h_bank%d" % i)
-            for t in range(PACK):
-                nc.scalar.activation(out=h_rows[t][:, cols], in_=views[t], func=ACT.Relu)
+            if i == 0:
+                outs = [first_banks[t // 2][:, t % 2, :] for t in range(PACK)]
+            else:
+                outs = [second_banks[t][:, c0 - 256 : c0 - 256 + n] for t in range(PACK)]
+            mix(outs, z_codes[:, cols], z_scales[:, cols], w1d, w1sd)
+            if i == 0:
+                for t in range(PACK):
+                    nc.scalar.activation(out=h_rows[t][:, cols], in_=outs[t], func=ACT.Relu)
+        for t in range(PACK):
+            nc.scalar.activation(out=h_rows[t][:, 256:512], in_=second_banks[t][:], func=ACT.Relu)
 
-        w2d = deal_words([w2w], "w2d", "z_woven2")
+        w2d = deal(w2w, "w2d", U8, 2, "z_space")
 
         z2_codes = sb([P, D], U32, "z2_codes")
         z2_scales = sb([P, D], U8, "z2_scales")
@@ -221,8 +210,9 @@ def tile_picked_mixdeep_relu_po_kernel(
             else:
                 woven = weave("scalar", z2_planes[:], "z2_woven%d" % i, tag="ring%d" % (i % 2))
             quantize(woven, z2_codes[:, cols], z2_scales[:, cols])
-            banks, views = mix(z2_codes[:, cols], z2_scales[:, cols], n, w2d, w2sd, (7, 4, 5, 6)[i], PACK, "o_bank%d" % i)
-            o_banks.append(banks[0])
+            bank = psum.tile([P, PACK, n], F32, name="o_bank%d" % i, tag="bank%d" % (6, 7, 4, 5)[i])
+            mix([bank[:, t, :] for t in range(PACK)], z2_codes[:, cols], z2_scales[:, cols], w2d, w2sd)
+            o_banks.append(bank)
 
         def finish(i, tag, parts, store_from):
             c0, n = OUT_CHUNKS[i]

@@ -20,7 +20,7 @@ T = 2048
 QUADS = 4
 FLOPS = 3 * 2 * D * D * D
 
-WA_CHUNKS = ((0, 128), (128, 128), (256, 128), (384, 128))
+WA_CHUNKS = ((0, 384), (384, 128))
 WA_QUANT = ((0, 256), (256, 128), (384, 128))
 Z_CHUNKS = ((0, 256), (256, 128), (384, 128))
 OUT_CHUNKS = ((0, 128), (128, 128), (256, 128), (384, 128))
@@ -90,11 +90,15 @@ def tile_picked_mixdeep_relu_po_kernel(
         nc.sync.dma_start(out=xw[:].bitcast(I32), in_=x_words[0].rearrange("p n t -> p (n t)").bitcast(I32))
         nc.sync.dma_start(fl_t[:], fl)
         nc.sync.dma_start(fm_t[:], fm)
-        nc.gpsimd.dma_start(out=ws[96:112, :].bitcast(I32), in_=w1_scales[0].bitcast(I32))
-        nc.gpsimd.dma_start(out=ws[112:128, :].bitcast(I32), in_=w2_scales[0].bitcast(I32))
+        nc.sync.dma_start(out=ws[96:112, :].bitcast(I32), in_=w1_scales[0].bitcast(I32))
+        nc.sync.dma_start(out=ws[112:128, :].bitcast(I32), in_=w2_scales[0].bitcast(I32))
         wa_rows = wa.rearrange("(p t) n -> p t n", t=PACK)
         wa_raw = []
-        for c0, n in WA_CHUNKS:
+        gt_t = sb([P, PACK], F32, "gt_t")
+        gp_t = sb([P, PACK], F32, "gp_t")
+        nc.gpsimd.dma_start(out=gt_t[:], in_=gt.rearrange("(p t) o -> p (t o)", t=PACK))
+        nc.gpsimd.dma_start(out=gp_t[:], in_=gp.rearrange("(p t) o -> p (t o)", t=PACK))
+        for c0, n in WA_CHUNKS[:-1]:
             raw = sb([P, PACK, n], F32, "wa_raw%d" % c0)
             nc.sync.dma_start(out=raw[:], in_=wa_rows[:, :, c0 : c0 + n])
             wa_raw.append(raw[:])
@@ -104,45 +108,53 @@ def tile_picked_mixdeep_relu_po_kernel(
         xs_staged = deal(xs_picked, "xs_staged", U8, 1)
         place_scale_rows(xs_plane, xs_staged, 112)
         xs_dealt = xs_plane
-        gt_t = sb([P, PACK], F32, "gt_t", "xs_picked")
-        nc.sync.dma_start(out=gt_t[:], in_=gt.rearrange("(p t) o -> p (t o)", t=PACK))
+        c0, n = WA_CHUNKS[-1]
+        raw = sb([P, PACK, n], F32, "wa_raw%d" % c0, "xs_picked")
+        nc.sync.dma_start(out=raw[:], in_=wa_rows[:, :, c0 : c0 + n])
+        wa_raw.append(raw[:])
         xw_dealt = sb([P, D], U32, "xw_dealt")
         nc.vector.tensor_copy(out=xw_dealt[:].rearrange("p (t m) -> p m t", t=PACK), in_=xw[:].indirect(offs_t[:]))
-        ws_staged = deal(ws, "ws_staged", U8, 1, "xw")
-        w1w = sb([P, 2 * D], U8, "w1w", "wa_raw0")
+        ws_staged = deal(ws, "ws_staged", U8, 1)
+        w1w = sb([P, 2 * D], U8, "w1w", "xw")
         nc.sync.dma_start(out=w1w[:].bitcast(I32), in_=w1_words[0].bitcast(I32))
         w1sd = ws_planes[:, 0:D]
         w2sd = ws_planes[:, D : 2 * D]
         place_scale_rows(w1sd, ws_staged, 96)
         place_scale_rows(w2sd, ws_staged, 112)
-        w2w = sb([P, 2 * D], U8, "w2w", "wa_raw128")
+        w2w = sb([P, 2 * D], U8, "w2w", "wa_raw0")
         nc.sync.dma_start(out=w2w[:].bitcast(I32), in_=w2_words[0].bitcast(I32))
-        gp_t = sb([P, PACK], F32, "gp_t", "wa_raw256")
-        nc.sync.dma_start(out=gp_t[:], in_=gp.rearrange("(p t) o -> p (t o)", t=PACK))
-        res_t = sb([P, PACK, D], F32, "res_t", "wa_raw384")
+        res_t = sb([P, PACK, D], F32, "res_t", "ws")
         nc.sync.dma_start(out=res_t[:], in_=res.rearrange("(p t) n -> p t n", t=PACK))
 
         y_banks = [psum.tile([P, D], F32, name="y_bank%d" % t, tag="bank%d" % t) for t in range(PACK)]
+        y_late = psum.tile([P, P], F32, name="y_late", tag="bank6")
         wa_woven = [sb([P, n, PACK], BF16, "wa_woven%d" % i) for i, (c0, n) in enumerate(WA_QUANT)]
-        weave_into("scalar", wa_raw[0], wa_woven[0][:, 0:128, :], True)
-        weave_into("scalar", wa_raw[1], wa_woven[0][:, 128:256, :])
-        weave_into("scalar", wa_raw[2], wa_woven[1][:])
-        weave_into("vector", wa_raw[3], wa_woven[2][:])
+        weave_into("scalar", wa_raw[0][:, :, 0:256], wa_woven[0][:], True)
+        weave_into("vector", wa_raw[0][:, :, 256:384], wa_woven[1][:])
+        weave_into("vector", wa_raw[1], wa_woven[2][:])
         wa_codes = sb([P, D], U32, "wa_codes")
         wa_scales = sb([P, D], U8, "wa_scales")
         for i, (c0, n) in enumerate(WA_QUANT):
             cols = slice(c0, c0 + n)
             quantize(wa_woven[i][:], wa_codes[:, cols], wa_scales[:, cols])
-        for t in range(PACK):
-            for c0, n in WA_QUANT if t == 0 else ((0, D),):
-                cols = slice(c0, c0 + n)
-                m = slice(t * P, (t + 1) * P)
-                nc.tensor.matmul_mx(
-                    out=y_banks[t][:, cols], lhsT=xw_dealt[:, m].bitcast(FP8X4), lhsT_scale=xs_dealt[:, m],
-                    rhs=wa_codes[:, cols].bitcast(FP8X4), rhs_scale=wa_scales[:, cols], start=True, stop=True,
-                )
+        def project(t, c0, n, out):
+            m = slice(t * P, (t + 1) * P)
+            nc.tensor.matmul_mx(
+                out=out, lhsT=xw_dealt[:, m].bitcast(FP8X4), lhsT_scale=xs_dealt[:, m],
+                rhs=wa_codes[:, c0 : c0 + n].bitcast(FP8X4), rhs_scale=wa_scales[:, c0 : c0 + n], start=True, stop=True,
+            )
+
         y_rows = [sb([P, D], F32, "y_rows%d" % t) for t in range(PACK)]
-        for t in range(PACK):
+        project(0, 0, 256, y_banks[0][:, 0:256])
+        project(0, 256, 128, y_banks[0][:, 256:384])
+        project(0, 384, 128, y_late[:])
+        nc.scalar.activation(out=y_rows[0][:, 0:384], in_=y_banks[0][:, 0:384], func=ACT.Copy, scale=gt_t[:, 0:1])
+        nc.scalar.activation(out=y_rows[0][:, 384:512], in_=y_late[:], func=ACT.Copy, scale=gt_t[:, 0:1])
+        project(1, 0, 256, y_banks[1][:, 0:256])
+        project(1, 256, 256, y_banks[1][:, 256:512])
+        for t in range(2, PACK):
+            project(t, 0, D, y_banks[t][:])
+        for t in range(1, PACK):
             nc.scalar.activation(out=y_rows[t][:], in_=y_banks[t][:], func=ACT.Copy, scale=gt_t[:, t : t + 1])
 
         w1d = deal(w1w, "w1d", U8, 2, "wa_woven2")
@@ -193,7 +205,7 @@ def tile_picked_mixdeep_relu_po_kernel(
         out_rows = out_0.rearrange("(p t) n -> p t n", t=PACK)
         out_words = out_1[0].rearrange("p n t -> p (n t)").bitcast(I32)
         o_banks = []
-        h_space = [sb([P, D], F32, "h_space%d" % i) for i in range(2)]
+        h_space = []
         for i, (c0, n) in enumerate(OUT_CHUNKS):
             cols = slice(c0, c0 + n)
             if i < 2:
@@ -205,7 +217,8 @@ def tile_picked_mixdeep_relu_po_kernel(
                 nc.vector.tensor_copy(out=h_planes[:, t, :], in_=h_rows[t][:].indirect(fm_t[:, c0 // 16 : (c0 + n) // 16]))
                 nc.scalar.activation(out=z2_planes[:, t, :], in_=h_planes[:, t, :], func=ACT.Copy, scale=gp_t[:, t : t + 1])
             if i < 2:
-                woven = h_space[i][:, n : 3 * n].bitcast(BF16).rearrange("p (n t) -> p n t", t=PACK)
+                h_space.append(sb([P, D], F32, "h_space%d" % i, "z2_planes0" if i == 1 else None))
+                woven = h_space[i][:, 240:496].bitcast(BF16).rearrange("p (n t) -> p n t", t=PACK)
                 weave_into("scalar", z2_planes[:], woven)
             else:
                 woven = weave("scalar", z2_planes[:], "z2_woven%d" % i, tag="ring%d" % (i % 2))

@@ -20,8 +20,8 @@ T = 2048
 QUADS = 4
 FLOPS = 3 * 2 * D * D * D
 
-WA_CHUNKS = ((0, 384), (384, 128))
-WA_QUANT = ((0, 256), (256, 128), (384, 128))
+WA_CHUNKS = ((0, 128), (128, 256), (384, 128))
+WA_QUANT = WA_CHUNKS
 Z_CHUNKS = ((0, 256), (256, 128), (384, 128))
 OUT_CHUNKS = ((0, 128), (128, 128), (256, 128), (384, 128))
 
@@ -123,15 +123,16 @@ def tile_picked_mixdeep_relu_po_kernel(
         place_scale_rows(w2sd, ws_staged, 112)
         w2w = sb([P, 2 * D], U8, "w2w", "wa_raw0")
         nc.sync.dma_start(out=w2w[:].bitcast(I32), in_=w2_words[0].bitcast(I32))
-        res_t = sb([P, PACK, D], F32, "res_t", "ws")
+        res_t = sb([P, PACK, D], F32, "res_t", "wa_raw128")
         nc.sync.dma_start(out=res_t[:], in_=res.rearrange("(p t) n -> p t n", t=PACK))
 
         y_banks = [psum.tile([P, D], F32, name="y_bank%d" % t, tag="bank%d" % t) for t in range(PACK)]
         y_late = psum.tile([P, P], F32, name="y_late", tag="bank6")
         wa_woven = [sb([P, n, PACK], BF16, "wa_woven%d" % i) for i, (c0, n) in enumerate(WA_QUANT)]
-        weave_into("scalar", wa_raw[0][:, :, 0:256], wa_woven[0][:], True)
-        weave_into("vector", wa_raw[0][:, :, 256:384], wa_woven[1][:])
-        weave_into("vector", wa_raw[1], wa_woven[2][:])
+        weave_into("scalar", wa_raw[0], wa_woven[0][:], True)
+        weave_into("scalar", wa_raw[1][:, :, 0:128], wa_woven[1][:, 0:128, :])
+        weave_into("vector", wa_raw[1][:, :, 128:256], wa_woven[1][:, 128:256, :])
+        weave_into("vector", wa_raw[2], wa_woven[2][:])
         wa_codes = sb([P, D], U32, "wa_codes")
         wa_scales = sb([P, D], U8, "wa_scales")
         for i, (c0, n) in enumerate(WA_QUANT):
@@ -145,14 +146,12 @@ def tile_picked_mixdeep_relu_po_kernel(
             )
 
         y_rows = [sb([P, D], F32, "y_rows%d" % t) for t in range(PACK)]
-        project(0, 0, 256, y_banks[0][:, 0:256])
-        project(0, 256, 128, y_banks[0][:, 256:384])
+        project(0, 0, 128, y_banks[0][:, 0:128])
+        project(0, 128, 256, y_banks[0][:, 128:384])
         project(0, 384, 128, y_late[:])
         nc.scalar.activation(out=y_rows[0][:, 0:384], in_=y_banks[0][:, 0:384], func=ACT.Copy, scale=gt_t[:, 0:1])
         nc.scalar.activation(out=y_rows[0][:, 384:512], in_=y_late[:], func=ACT.Copy, scale=gt_t[:, 0:1])
-        project(1, 0, 256, y_banks[1][:, 0:256])
-        project(1, 256, 256, y_banks[1][:, 256:512])
-        for t in range(2, PACK):
+        for t in range(1, PACK):
             project(t, 0, D, y_banks[t][:])
         for t in range(1, PACK):
             nc.scalar.activation(out=y_rows[t][:], in_=y_banks[t][:], func=ACT.Copy, scale=gt_t[:, t : t + 1])
@@ -217,8 +216,8 @@ def tile_picked_mixdeep_relu_po_kernel(
                 nc.vector.tensor_copy(out=h_planes[:, t, :], in_=h_rows[t][:].indirect(fm_t[:, c0 // 16 : (c0 + n) // 16]))
                 nc.scalar.activation(out=z2_planes[:, t, :], in_=h_planes[:, t, :], func=ACT.Copy, scale=gp_t[:, t : t + 1])
             if i < 2:
-                h_space.append(sb([P, D], F32, "h_space%d" % i, "z2_planes0" if i == 1 else None))
-                woven = h_space[i][:, 240:496].bitcast(BF16).rearrange("p (n t) -> p n t", t=PACK)
+                h_space.append(sb([P, D], F32, "h_space%d" % i))
+                woven = h_space[i][:, n : 3 * n].bitcast(BF16).rearrange("p (n t) -> p n t", t=PACK)
                 weave_into("scalar", z2_planes[:], woven)
             else:
                 woven = weave("scalar", z2_planes[:], "z2_woven%d" % i, tag="ring%d" % (i % 2))

@@ -18,12 +18,15 @@ PACK = 4
 D = 512
 T = 2048
 QUADS = 4
+SCALE_ROWS = 16
+PER_COLUMN = 16
 FLOPS = 3 * 2 * D * D * D
 
-WA_CHUNKS = ((0, 128), (128, 256), (384, 128))
-WA_QUANT = WA_CHUNKS
-Z_CHUNKS = ((0, 256), (256, 128), (384, 128))
-OUT_CHUNKS = ((0, 128), (128, 128), (256, 128), (384, 128))
+WA_EARLY, WA_LATE = (0, 384), (384, 128)
+WA_PIECES = ((0, 128), (128, 256), (384, 128))
+Z_PIECES = ((0, 256), (256, 128), (384, 128))
+OUT_WIDTH = 128
+OUT_PIECES = D // OUT_WIDTH
 
 
 def tile_picked_mixdeep_relu_po_kernel(
@@ -35,220 +38,242 @@ def tile_picked_mixdeep_relu_po_kernel(
         keep = ctx.enter_context(tc.tile_pool(name="keep", bufs=1))
         psum = ctx.enter_context(tc.psum_pool(name="psum", bufs=1))
 
-        def sb(shape, dtype, name, tag=None):
-            return keep.tile(shape, dtype, name=name, tag=tag or name, align_bytes=64)
+        def sbuf(shape, dtype, name, reuses=None):
+            return keep.tile(shape, dtype, name=name, tag=reuses or name, align_bytes=64)
 
-        def place_scale_rows(plane, staged, first):
-            for q in range(QUADS):
-                nc.sync.dma_start(
-                    out=plane[32 * q : 32 * q + 4, :].bitcast(I32),
-                    in_=staged[first + 4 * q : first + 4 * q + 4, :].bitcast(I32),
-                )
+        def bank(shape, name, number):
+            return psum.tile(shape, F32, name=name, tag="bank%d" % number)
 
-        def weave(engine, planes, name, as_activation=False, tag=None):
-            woven = sb([P, planes.shape[2], PACK], BF16, name, tag)
-            weave_into(engine, planes, woven[:], as_activation)
-            return woven[:]
+        def weave_views(planes, woven):
+            return woven.rearrange("p (c i) t -> p c t i", i=4), planes.rearrange("p t (c i) -> p c t i", i=4)
 
-        def weave_into(engine, planes, woven, as_activation=False):
-            dst = woven.rearrange("p (c i) t -> p c t i", i=4)
-            src = planes.rearrange("p t (c i) -> p c t i", i=4)
-            if as_activation:
-                nc.scalar.activation(out=dst, in_=src, func=ACT.Copy)
-            elif engine == "scalar":
-                nc.scalar.copy(out=dst, in_=src)
-            else:
-                nc.vector.tensor_copy(out=dst, in_=src)
+        def weave_on_scalar(planes, woven):
+            dst, src = weave_views(planes, woven)
+            nc.scalar.copy(out=dst, in_=src)
+
+        def weave_on_vector(planes, woven):
+            dst, src = weave_views(planes, woven)
+            nc.vector.tensor_copy(out=dst, in_=src)
 
         def quantize(woven, codes, scales):
             nc.vector.quantize_mx(out=codes.bitcast(FP8X4), scales=scales, in_=woven.rearrange("p n t -> p (n t)"))
 
-        def deal(words, name, dtype, width, tag=None):
-            dealt = sb([P, width * D], dtype, name, tag)
+        def deal(source, name, column_bytes, reuses=None):
+            dealt = sbuf([P, column_bytes * D], U8, name, reuses)
             nc.vector.tensor_copy(
-                out=dealt[:].rearrange("p (t m b) -> p t m b", t=PACK, b=width),
-                in_=words[:].rearrange("p (m t b) -> p t m b", t=PACK, b=width),
+                out=dealt[:].rearrange("p (t m b) -> p t m b", t=PACK, b=column_bytes),
+                in_=source[:].rearrange("p (m t b) -> p t m b", t=PACK, b=column_bytes),
             )
             return dealt
 
-        offs_t = lists.tile([P, D // 16], U16, name="offs_t")
-        fl_t = lists.tile([P, D // 16], U16, name="fl_t")
-        fm_t = lists.tile([P, D // 16], U16, name="fm_t")
-        xs = sb([P, T], U8, "xs")
-        xw = sb([P, T], U32, "xw")
-        ws = sb([P, D], U8, "ws")
-        xs_plane = sb([P, D], U8, "xs_plane")
-        ws_planes = sb([P, 2 * D], U8, "ws_planes")
+        def place_scale_rows(scales, staged, first):
+            for q in range(QUADS):
+                nc.sync.dma_start(
+                    out=scales[32 * q : 32 * q + 4, :].bitcast(I32),
+                    in_=staged[first + 4 * q : first + 4 * q + 4, :].bitcast(I32),
+                )
 
-        nc.vector.memset(xs[0:112, :].bitcast(I32), 0)
-        nc.vector.memset(ws[0:96, :].bitcast(I32), 0)
-        nc.vector.memset(xs_plane[:].bitcast(I32), 0)
-        nc.vector.memset(ws_planes[:].bitcast(I32), 0)
+        def entries(list_tile, first, count):
+            return list_tile[:, first // PER_COLUMN : (first + count) // PER_COLUMN]
+
+        last_rows = P - SCALE_ROWS
+        w1_rows = P - 2 * SCALE_ROWS
+        offs_t = lists.tile([P, D // PER_COLUMN], U16, name="offs_t")
+        fl_t = lists.tile([P, D // PER_COLUMN], U16, name="fl_t")
+        fm_t = lists.tile([P, D // PER_COLUMN], U16, name="fm_t")
+        xs_table = sbuf([P, T], U8, "xs_table")
+        xw_table = sbuf([P, T], U32, "xw_table")
+        ws_raw = sbuf([P, D], U8, "ws_raw")
+        x_scale = sbuf([P, D], U8, "x_scale")
+        w_scales = sbuf([P, 2 * D], U8, "w_scales")
+
+        nc.vector.memset(xs_table[0:last_rows, :].bitcast(I32), 0)
+        nc.vector.memset(ws_raw[0:w1_rows, :].bitcast(I32), 0)
+        nc.vector.memset(x_scale[:].bitcast(I32), 0)
+        nc.vector.memset(w_scales[:].bitcast(I32), 0)
 
         nc.sync.dma_start(offs_t[:], offs)
-        nc.sync.dma_start(out=xs[112:128, :].bitcast(I32), in_=x_scales[0].bitcast(I32))
-        nc.sync.dma_start(out=xw[:].bitcast(I32), in_=x_words[0].rearrange("p n t -> p (n t)").bitcast(I32))
+        nc.sync.dma_start(out=xs_table[last_rows:P, :].bitcast(I32), in_=x_scales[0].bitcast(I32))
+        nc.sync.dma_start(out=xw_table[:].bitcast(I32), in_=x_words[0].rearrange("p n t -> p (n t)").bitcast(I32))
         nc.sync.dma_start(fl_t[:], fl)
         nc.sync.dma_start(fm_t[:], fm)
-        nc.sync.dma_start(out=ws[96:112, :].bitcast(I32), in_=w1_scales[0].bitcast(I32))
-        nc.sync.dma_start(out=ws[112:128, :].bitcast(I32), in_=w2_scales[0].bitcast(I32))
-        wa_rows = wa.rearrange("(p t) n -> p t n", t=PACK)
-        wa_raw = []
-        gt_t = sb([P, PACK], F32, "gt_t")
-        gp_t = sb([P, PACK], F32, "gp_t")
+        nc.sync.dma_start(out=ws_raw[w1_rows:last_rows, :].bitcast(I32), in_=w1_scales[0].bitcast(I32))
+        nc.sync.dma_start(out=ws_raw[last_rows:P, :].bitcast(I32), in_=w2_scales[0].bitcast(I32))
+        gt_t = sbuf([P, PACK], F32, "gt_t")
+        gp_t = sbuf([P, PACK], F32, "gp_t")
         nc.gpsimd.dma_start(out=gt_t[:], in_=gt.rearrange("(p t) o -> p (t o)", t=PACK))
         nc.gpsimd.dma_start(out=gp_t[:], in_=gp.rearrange("(p t) o -> p (t o)", t=PACK))
-        for c0, n in WA_CHUNKS[:-1]:
-            raw = sb([P, PACK, n], F32, "wa_raw%d" % c0)
-            nc.sync.dma_start(out=raw[:], in_=wa_rows[:, :, c0 : c0 + n])
-            wa_raw.append(raw[:])
+        wa_planes = wa.rearrange("(p t) n -> p t n", t=PACK)
+        wa_early = sbuf([P, PACK, WA_EARLY[1]], F32, "wa_early")
+        nc.sync.dma_start(out=wa_early[:], in_=wa_planes[:, :, 0 : WA_EARLY[1]])
 
-        xs_picked = sb([P, D], U8, "xs_picked")
-        nc.vector.tensor_copy(out=xs_picked[:], in_=xs[:].indirect(offs_t[:]))
-        xs_staged = deal(xs_picked, "xs_staged", U8, 1)
-        place_scale_rows(xs_plane, xs_staged, 112)
-        xs_dealt = xs_plane
-        c0, n = WA_CHUNKS[-1]
-        raw = sb([P, PACK, n], F32, "wa_raw%d" % c0, "xs_picked")
-        nc.sync.dma_start(out=raw[:], in_=wa_rows[:, :, c0 : c0 + n])
-        wa_raw.append(raw[:])
-        xw_dealt = sb([P, D], U32, "xw_dealt")
-        nc.vector.tensor_copy(out=xw_dealt[:].rearrange("p (t m) -> p m t", t=PACK), in_=xw[:].indirect(offs_t[:]))
-        ws_staged = deal(ws, "ws_staged", U8, 1)
-        w1w = sb([P, 2 * D], U8, "w1w", "xw")
-        nc.sync.dma_start(out=w1w[:].bitcast(I32), in_=w1_words[0].bitcast(I32))
-        w1sd = ws_planes[:, 0:D]
-        w2sd = ws_planes[:, D : 2 * D]
-        place_scale_rows(w1sd, ws_staged, 96)
-        place_scale_rows(w2sd, ws_staged, 112)
-        w2w = sb([P, 2 * D], U8, "w2w", "wa_raw0")
-        nc.sync.dma_start(out=w2w[:].bitcast(I32), in_=w2_words[0].bitcast(I32))
-        res_t = sb([P, PACK, D], F32, "res_t", "wa_raw128")
-        nc.sync.dma_start(out=res_t[:], in_=res.rearrange("(p t) n -> p t n", t=PACK))
+        xs_picked = sbuf([P, D], U8, "xs_picked")
+        nc.vector.tensor_copy(out=xs_picked[:], in_=xs_table[:].indirect(offs_t[:]))
+        xs_staged = deal(xs_picked, "xs_staged", 1)
+        place_scale_rows(x_scale, xs_staged, last_rows)
+        wa_late = sbuf([P, PACK, WA_LATE[1]], F32, "wa_late", "xs_picked")
+        nc.sync.dma_start(out=wa_late[:], in_=wa_planes[:, :, WA_LATE[0] : D])
+        x_codes = sbuf([P, D], U32, "x_codes")
+        nc.vector.tensor_copy(out=x_codes[:].rearrange("p (t m) -> p m t", t=PACK), in_=xw_table[:].indirect(offs_t[:]))
 
-        y_banks = [psum.tile([P, D], F32, name="y_bank%d" % t, tag="bank%d" % t) for t in range(PACK)]
-        y_late = psum.tile([P, P], F32, name="y_late", tag="bank6")
-        wa_woven = [sb([P, n, PACK], BF16, "wa_woven%d" % i) for i, (c0, n) in enumerate(WA_QUANT)]
-        weave_into("scalar", wa_raw[0], wa_woven[0][:], True)
-        weave_into("scalar", wa_raw[1][:, :, 0:128], wa_woven[1][:, 0:128, :])
-        weave_into("vector", wa_raw[1][:, :, 128:256], wa_woven[1][:, 128:256, :])
-        weave_into("vector", wa_raw[2], wa_woven[2][:])
-        wa_codes = sb([P, D], U32, "wa_codes")
-        wa_scales = sb([P, D], U8, "wa_scales")
-        for i, (c0, n) in enumerate(WA_QUANT):
-            cols = slice(c0, c0 + n)
-            quantize(wa_woven[i][:], wa_codes[:, cols], wa_scales[:, cols])
-        def project(t, c0, n, out):
-            m = slice(t * P, (t + 1) * P)
+        ws_staged = deal(ws_raw, "ws_staged", 1)
+        w1_raw = sbuf([P, 2 * D], U8, "w1_raw", "xw_table")
+        nc.sync.dma_start(out=w1_raw[:].bitcast(I32), in_=w1_words[0].bitcast(I32))
+        w1_scale = w_scales[:, 0:D]
+        w2_scale = w_scales[:, D : 2 * D]
+        place_scale_rows(w1_scale, ws_staged, w1_rows)
+        place_scale_rows(w2_scale, ws_staged, last_rows)
+        w2_raw = sbuf([P, 2 * D], U8, "w2_raw", "ws_raw")
+        nc.sync.dma_start(out=w2_raw[:].bitcast(I32), in_=w2_words[0].bitcast(I32))
+        res_planes = sbuf([P, PACK, D], F32, "res_planes", "wa_early")
+        nc.sync.dma_start(out=res_planes[:], in_=res.rearrange("(p t) n -> p t n", t=PACK))
+
+        y_banks = [bank([P, D], "y_bank%d" % t, t) for t in range(PACK)]
+        y_late = bank([P, WA_LATE[1]], "y_late", 6)
+        wa_woven = [sbuf([P, n, PACK], BF16, "wa_woven%d" % i) for i, (first, n) in enumerate(WA_PIECES)]
+        on_scalar = WA_PIECES[0][1]
+        dst, src = weave_views(wa_early[:, :, 0:on_scalar], wa_woven[0][:])
+        nc.scalar.activation(out=dst, in_=src, func=ACT.Copy)
+        weave_on_vector(wa_early[:, :, on_scalar : WA_EARLY[1]], wa_woven[1][:])
+        weave_on_vector(wa_late[:], wa_woven[2][:])
+        wa_codes = sbuf([P, D], U32, "wa_codes")
+        wa_scale = sbuf([P, D], U8, "wa_scale")
+        for i, (first, n) in enumerate(WA_PIECES):
+            quantize(wa_woven[i][:], wa_codes[:, first : first + n], wa_scale[:, first : first + n])
+
+        def project(t, first, n, out):
+            tokens = slice(t * P, (t + 1) * P)
             nc.tensor.matmul_mx(
-                out=out, lhsT=xw_dealt[:, m].bitcast(FP8X4), lhsT_scale=xs_dealt[:, m],
-                rhs=wa_codes[:, c0 : c0 + n].bitcast(FP8X4), rhs_scale=wa_scales[:, c0 : c0 + n], start=True, stop=True,
+                out=out,
+                lhsT=x_codes[:, tokens].bitcast(FP8X4),
+                lhsT_scale=x_scale[:, tokens],
+                rhs=wa_codes[:, first : first + n].bitcast(FP8X4),
+                rhs_scale=wa_scale[:, first : first + n],
+                start=True,
+                stop=True,
             )
 
-        y_rows = [sb([P, D], F32, "y_rows%d" % t) for t in range(PACK)]
-        project(0, 0, 128, y_banks[0][:, 0:128])
-        project(0, 128, 256, y_banks[0][:, 128:384])
-        project(0, 384, 128, y_late[:])
-        nc.scalar.activation(out=y_rows[0][:, 0:384], in_=y_banks[0][:, 0:384], func=ACT.Copy, scale=gt_t[:, 0:1])
-        nc.scalar.activation(out=y_rows[0][:, 384:512], in_=y_late[:], func=ACT.Copy, scale=gt_t[:, 0:1])
+        y_planes = [sbuf([P, D], F32, "y_plane%d" % t) for t in range(PACK)]
+        for first, n in WA_PIECES[:-1]:
+            project(0, first, n, y_banks[0][:, first : first + n])
+        project(0, WA_LATE[0], WA_LATE[1], y_late[:])
+        early = slice(0, WA_EARLY[1])
+        nc.scalar.activation(out=y_planes[0][:, early], in_=y_banks[0][:, early], func=ACT.Copy, scale=gt_t[:, 0:1])
+        nc.scalar.activation(out=y_planes[0][:, WA_LATE[0] : D], in_=y_late[:], func=ACT.Copy, scale=gt_t[:, 0:1])
         for t in range(1, PACK):
             project(t, 0, D, y_banks[t][:])
         for t in range(1, PACK):
-            nc.scalar.activation(out=y_rows[t][:], in_=y_banks[t][:], func=ACT.Copy, scale=gt_t[:, t : t + 1])
+            nc.scalar.activation(out=y_planes[t][:], in_=y_banks[t][:], func=ACT.Copy, scale=gt_t[:, t : t + 1])
 
-        w1d = deal(w1w, "w1d", U8, 2, "wa_woven2")
+        w1_codes = deal(w1_raw, "w1_codes", 2, "wa_woven2")
 
-        def mix(outs, codes, scales, words, wscales):
+        def mix(outs, w_codes, w_scale, codes, scale):
             for t in range(PACK):
                 nc.tensor.matmul_mx(
-                    out=outs[t], lhsT=words[:, 2 * P * t : 2 * P * (t + 1)].bitcast(FP4X4),
-                    lhsT_scale=wscales[:, P * t : P * (t + 1)],
-                    rhs=codes.bitcast(FP8X4), rhs_scale=scales, start=True, stop=True,
+                    out=outs[t],
+                    lhsT=w_codes[:, 2 * P * t : 2 * P * (t + 1)].bitcast(FP4X4),
+                    lhsT_scale=w_scale[:, P * t : P * (t + 1)],
+                    rhs=codes.bitcast(FP8X4),
+                    rhs_scale=scale,
+                    start=True,
+                    stop=True,
                 )
 
-        h_rows = [sb([P, D], F32, "h_rows%d" % t) for t in range(PACK)]
-        z_space = sb([P, 1920], BF16, "z_space")
-        z_codes = sb([P, D], U32, "z_codes")
-        z_scales = sb([P, D], U8, "z_scales")
-        first_banks = [psum.tile([P, 2, 256], F32, name="h_first%d" % b, tag="bank%d" % (4 + b)) for b in range(2)]
-        second_banks = [psum.tile([P, 256], F32, name="h_second%d" % t, tag="bank%d" % t) for t in range(PACK)]
-        for i, (c0, n) in enumerate(Z_CHUNKS):
-            cols = slice(c0, c0 + n)
-            if i < 2:
-                z_planes = sb([P, PACK, n], BF16, "z_planes%d" % i)[:]
+        half = Z_PIECES[0][1]
+        plane_stride = 384
+        woven_at = (plane_stride, plane_stride + PACK * half, plane_stride + PACK * half)
+        h_planes = [sbuf([P, D], F32, "h_plane%d" % t) for t in range(PACK)]
+        z_shared = sbuf([P, woven_at[2] + PACK * Z_PIECES[2][1]], BF16, "z_shared")
+        z_codes = sbuf([P, D], U32, "z_codes")
+        z_scale = sbuf([P, D], U8, "z_scale")
+        first_half = [bank([P, 2, half], "h_first%d" % b, PACK + b) for b in range(2)]
+        second_half = [bank([P, half], "h_second%d" % t, t) for t in range(PACK)]
+        for i, (first, n) in enumerate(Z_PIECES):
+            cols = slice(first, first + n)
+            is_last = i == len(Z_PIECES) - 1
+            if is_last:
+                z_piece = z_shared[:, 0 : PACK * plane_stride].rearrange("p (t n) -> p t n", t=PACK)[:, :, 0:n]
             else:
-                z_planes = z_space[:, 0:1536].rearrange("p (t n) -> p t n", t=PACK)[:, :, 0:n]
+                z_piece = sbuf([P, PACK, n], BF16, "z_piece%d" % i)[:]
             for t in range(PACK):
-                nc.vector.tensor_copy(out=z_planes[:, t, :], in_=y_rows[t][:].indirect(fl_t[:, c0 // 16 : (c0 + n) // 16]))
-            at = 384 if i == 0 else 1408
-            woven = z_space[:, at : at + PACK * n].rearrange("p (n t) -> p n t", t=PACK)
-            weave_into("scalar" if i < 2 else "vector", z_planes, woven)
-            quantize(woven, z_codes[:, cols], z_scales[:, cols])
-            if i == 0:
-                outs = [first_banks[t // 2][:, t % 2, :] for t in range(PACK)]
+                nc.vector.tensor_copy(out=z_piece[:, t, :], in_=y_planes[t][:].indirect(entries(fl_t, first, n)))
+            woven = z_shared[:, woven_at[i] : woven_at[i] + PACK * n].rearrange("p (n t) -> p n t", t=PACK)
+            if is_last:
+                weave_on_vector(z_piece, woven)
             else:
-                outs = [second_banks[t][:, c0 - 256 : c0 - 256 + n] for t in range(PACK)]
-            mix(outs, z_codes[:, cols], z_scales[:, cols], w1d, w1sd)
-            if i == 0:
+                weave_on_scalar(z_piece, woven)
+            quantize(woven, z_codes[:, cols], z_scale[:, cols])
+            if first < half:
+                outs = [first_half[t // 2][:, t % 2, :] for t in range(PACK)]
+            else:
+                outs = [second_half[t][:, first - half : first - half + n] for t in range(PACK)]
+            mix(outs, w1_codes, w1_scale, z_codes[:, cols], z_scale[:, cols])
+            if first < half:
                 for t in range(PACK):
-                    nc.scalar.activation(out=h_rows[t][:, cols], in_=outs[t], func=ACT.Relu)
+                    nc.scalar.activation(out=h_planes[t][:, cols], in_=outs[t], func=ACT.Relu)
         for t in range(PACK):
-            nc.scalar.activation(out=h_rows[t][:, 256:512], in_=second_banks[t][:], func=ACT.Relu)
+            nc.scalar.activation(out=h_planes[t][:, half:D], in_=second_half[t][:], func=ACT.Relu)
 
-        w2d = deal(w2w, "w2d", U8, 2, "z_space")
+        w2_codes = deal(w2_raw, "w2_codes", 2, "z_shared")
 
-        z2_codes = sb([P, D], U32, "z2_codes")
-        z2_scales = sb([P, D], U8, "z2_scales")
-        o_codes = sb([P, D], U32, "o_codes")
-        o_scales = sb([P, D], U8, "o_scales")
-        out_rows = out_0.rearrange("(p t) n -> p t n", t=PACK)
+        z2_codes = sbuf([P, D], U32, "z2_codes")
+        z2_scale = sbuf([P, D], U8, "z2_scale")
+        out_codes = sbuf([P, D], U32, "out_codes")
+        out_scale = sbuf([P, D], U8, "out_scale")
+        out_planes = out_0.rearrange("(p t) n -> p t n", t=PACK)
         out_words = out_1[0].rearrange("p n t -> p (n t)").bitcast(I32)
-        o_banks = []
-        h_space = []
-        for i, (c0, n) in enumerate(OUT_CHUNKS):
-            cols = slice(c0, c0 + n)
+        out_bank_numbers = (6, 7, 4, 5)
+        out_banks = []
+        h_shared = []
+        for i in range(OUT_PIECES):
+            first = i * OUT_WIDTH
+            cols = slice(first, first + OUT_WIDTH)
             if i < 2:
-                h_planes = sb([P, PACK, n], F32, "h_planes%d" % i)[:]
+                h_piece = sbuf([P, PACK, OUT_WIDTH], F32, "h_piece%d" % i)[:]
             else:
-                h_planes = h_space[i - 2][:].rearrange("p (t n) -> p t n", t=PACK)
-            z2_planes = sb([P, PACK, n], BF16, "z2_planes%d" % i)
+                h_piece = h_shared[i - 2][:].rearrange("p (t n) -> p t n", t=PACK)
+            z2_piece = sbuf([P, PACK, OUT_WIDTH], BF16, "z2_piece%d" % i)
             for t in range(PACK):
-                nc.vector.tensor_copy(out=h_planes[:, t, :], in_=h_rows[t][:].indirect(fm_t[:, c0 // 16 : (c0 + n) // 16]))
-                nc.scalar.activation(out=z2_planes[:, t, :], in_=h_planes[:, t, :], func=ACT.Copy, scale=gp_t[:, t : t + 1])
+                nc.vector.tensor_copy(out=h_piece[:, t, :], in_=h_planes[t][:].indirect(entries(fm_t, first, OUT_WIDTH)))
+                nc.scalar.activation(out=z2_piece[:, t, :], in_=h_piece[:, t, :], func=ACT.Copy, scale=gp_t[:, t : t + 1])
             if i < 2:
-                h_space.append(sb([P, D], F32, "h_space%d" % i))
-                woven = h_space[i][:, n : 3 * n].bitcast(BF16).rearrange("p (n t) -> p n t", t=PACK)
-                weave_into("scalar", z2_planes[:], woven)
+                h_shared.append(sbuf([P, PACK * OUT_WIDTH], F32, "h_shared%d" % i))
+                woven = h_shared[i][:, OUT_WIDTH : 3 * OUT_WIDTH].bitcast(BF16).rearrange("p (n t) -> p n t", t=PACK)
             else:
-                woven = weave("scalar", z2_planes[:], "z2_woven%d" % i, tag="ring%d" % (i % 2))
-            quantize(woven, z2_codes[:, cols], z2_scales[:, cols])
-            bank = psum.tile([P, PACK, n], F32, name="o_bank%d" % i, tag="bank%d" % (6, 7, 4, 5)[i])
-            mix([bank[:, t, :] for t in range(PACK)], z2_codes[:, cols], z2_scales[:, cols], w2d, w2sd)
-            o_banks.append(bank)
+                woven = sbuf([P, OUT_WIDTH, PACK], BF16, "z2_woven%d" % i)[:]
+            weave_on_scalar(z2_piece[:], woven)
+            quantize(woven, z2_codes[:, cols], z2_scale[:, cols])
+            acc = bank([P, PACK, OUT_WIDTH], "out_bank%d" % i, out_bank_numbers[i])
+            mix([acc[:, t, :] for t in range(PACK)], w2_codes, w2_scale, z2_codes[:, cols], z2_scale[:, cols])
+            out_banks.append(acc)
 
-        def finish(i, tag, parts, store_from):
-            c0, n = OUT_CHUNKS[i]
-            o_planes = sb([P, PACK, n], F32, "o_planes%d" % i, tag)
-            o_woven = sb([P, n, PACK], BF16, "o_woven%d" % i)
-            w = n // parts
+        def finish(i, parts, reuses=None):
+            first = i * OUT_WIDTH
+            width = OUT_WIDTH // parts
+            total = sbuf([P, PACK, OUT_WIDTH], F32, "total%d" % i, reuses)
+            total_woven = sbuf([P, OUT_WIDTH, PACK], BF16, "total_woven%d" % i)
             for j in range(parts):
-                part = slice(j * w, (j + 1) * w)
-                cols = slice(c0 + j * w, c0 + (j + 1) * w)
-                nc.vector.tensor_tensor(out=o_planes[:, :, part], in0=o_banks[i][:, :, part], in1=res_t[:, :, cols], op=ALU.add)
-            nc.sync.dma_start(out=out_rows[:, :, c0 : c0 + n], in_=o_planes[:])
+                part = slice(j * width, (j + 1) * width)
+                cols = slice(first + j * width, first + (j + 1) * width)
+                nc.vector.tensor_tensor(out=total[:, :, part], in0=out_banks[i][:, :, part], in1=res_planes[:, :, cols], op=ALU.add)
+            nc.sync.dma_start(out=out_planes[:, :, first : first + OUT_WIDTH], in_=total[:])
             for j in range(parts):
-                part = slice(j * w, (j + 1) * w)
-                cols = slice(c0 + j * w, c0 + (j + 1) * w)
-                weave_into("scalar", o_planes[:, :, part], o_woven[:, part, :])
-                quantize(o_woven[:, part, :], o_codes[:, cols], o_scales[:, cols])
-            if store_from is not None:
-                cols = slice(store_from[0], store_from[1])
-                nc.sync.dma_start(out=out_words[:, cols], in_=o_codes[:, cols].bitcast(I32))
+                part = slice(j * width, (j + 1) * width)
+                cols = slice(first + j * width, first + (j + 1) * width)
+                weave_on_scalar(total[:, :, part], total_woven[:, part, :])
+                quantize(total_woven[:, part, :], out_codes[:, cols], out_scale[:, cols])
 
-        finish(1, None, 1, None)
-        finish(0, "ring0", 1, (0, 256))
-        finish(2, "ring1", 1, (256, 384))
-        finish(3, None, 2, (384, 512))
+        def store_words(first_piece, pieces):
+            cols = slice(first_piece * OUT_WIDTH, (first_piece + pieces) * OUT_WIDTH)
+            nc.sync.dma_start(out=out_words[:, cols], in_=out_codes[:, cols].bitcast(I32))
+
+        finish(1, 1)
+        finish(0, 1, "z2_woven2")
+        store_words(0, 2)
+        finish(2, 1, "z2_woven3")
+        store_words(2, 1)
+        finish(3, 2)
+        store_words(3, 1)
         for q in range(QUADS):
             queue = nc.sync if q % 2 == 0 else nc.scalar
-            queue.dma_start(out=out_2[0, 4 * q : 4 * q + 4, :].bitcast(I32), in_=o_scales[32 * q : 32 * q + 4, :].bitcast(I32))
+            queue.dma_start(out=out_2[0, 4 * q : 4 * q + 4, :].bitcast(I32), in_=out_scale[32 * q : 32 * q + 4, :].bitcast(I32))

from contextlib import ExitStack

import concourse.mybir as mybir

F32 = mybir.dt.float32
BF16 = mybir.dt.bfloat16
I32 = mybir.dt.int32
U32 = mybir.dt.uint32
U16 = mybir.dt.uint16
U8 = mybir.dt.uint8
FP8X4 = mybir.dt.float8_e4m3fn_x4
FP4X4 = mybir.dt.float4_e2m1fn_x4
ACT = mybir.ActivationFunctionType
ALU = mybir.AluOpType

P = 128
PACK = 4
D = 512
T = 2048
QUADS = 4
SCALE_ROWS = 16
PER_COLUMN = 16
FLOPS = 3 * 2 * D * D * D

WA_EARLY, WA_LATE = (0, 384), (384, 128)
WA_PIECES = ((0, 128), (128, 256), (384, 128))
Z_PIECES = ((0, 256), (256, 128), (384, 128))
OUT_WIDTH = 128
OUT_PIECES = D // OUT_WIDTH


def tile_picked_mixdeep_relu_po_kernel(
    tc, x_words, x_scales, wa, gt, w1_words, w1_scales, gp, res, w2_words, w2_scales, offs, fl, fm, out_0, out_1, out_2
):
    nc = tc.nc
    with ExitStack() as ctx:
        lists = ctx.enter_context(tc.tile_pool(name="lists", bufs=1))
        keep = ctx.enter_context(tc.tile_pool(name="keep", bufs=1))
        psum = ctx.enter_context(tc.psum_pool(name="psum", bufs=1))

        def sbuf(shape, dtype, name, reuses=None):
            return keep.tile(shape, dtype, name=name, tag=reuses or name, align_bytes=64)

        def bank(shape, name, number):
            return psum.tile(shape, F32, name=name, tag="bank%d" % number)

        def weave_views(planes, woven):
            return woven.rearrange("p (c i) t -> p c t i", i=4), planes.rearrange("p t (c i) -> p c t i", i=4)

        def weave_on_scalar(planes, woven):
            dst, src = weave_views(planes, woven)
            nc.scalar.copy(out=dst, in_=src)

        def weave_on_vector(planes, woven):
            dst, src = weave_views(planes, woven)
            nc.vector.tensor_copy(out=dst, in_=src)

        def quantize(woven, codes, scales):
            nc.vector.quantize_mx(out=codes.bitcast(FP8X4), scales=scales, in_=woven.rearrange("p n t -> p (n t)"))

        def deal(source, name, column_bytes, reuses=None):
            dealt = sbuf([P, column_bytes * D], U8, name, reuses)
            nc.vector.tensor_copy(
                out=dealt[:].rearrange("p (t m b) -> p t m b", t=PACK, b=column_bytes),
                in_=source[:].rearrange("p (m t b) -> p t m b", t=PACK, b=column_bytes),
            )
            return dealt

        def place_scale_rows(scales, staged, first):
            for q in range(QUADS):
                nc.sync.dma_start(
                    out=scales[32 * q : 32 * q + 4, :].bitcast(I32),
                    in_=staged[first + 4 * q : first + 4 * q + 4, :].bitcast(I32),
                )

        def entries(list_tile, first, count):
            return list_tile[:, first // PER_COLUMN : (first + count) // PER_COLUMN]

        last_rows = P - SCALE_ROWS
        w1_rows = P - 2 * SCALE_ROWS
        offs_t = lists.tile([P, D // PER_COLUMN], U16, name="offs_t")
        fl_t = lists.tile([P, D // PER_COLUMN], U16, name="fl_t")
        fm_t = lists.tile([P, D // PER_COLUMN], U16, name="fm_t")
        xs_table = sbuf([P, T], U8, "xs_table")
        xw_table = sbuf([P, T], U32, "xw_table")
        ws_raw = sbuf([P, D], U8, "ws_raw")
        x_scale = sbuf([P, D], U8, "x_scale")
        w_scales = sbuf([P, 2 * D], U8, "w_scales")

        nc.vector.memset(xs_table[0:last_rows, :].bitcast(I32), 0)
        nc.vector.memset(ws_raw[0:w1_rows, :].bitcast(I32), 0)
        nc.vector.memset(x_scale[:].bitcast(I32), 0)
        nc.vector.memset(w_scales[:].bitcast(I32), 0)

        nc.sync.dma_start(offs_t[:], offs)
        nc.sync.dma_start(out=xs_table[last_rows:P, :].bitcast(I32), in_=x_scales[0].bitcast(I32))
        nc.sync.dma_start(out=xw_table[:].bitcast(I32), in_=x_words[0].rearrange("p n t -> p (n t)").bitcast(I32))
        nc.sync.dma_start(fl_t[:], fl)
        nc.sync.dma_start(fm_t[:], fm)
        nc.sync.dma_start(out=ws_raw[w1_rows:last_rows, :].bitcast(I32), in_=w1_scales[0].bitcast(I32))
        nc.sync.dma_start(out=ws_raw[last_rows:P, :].bitcast(I32), in_=w2_scales[0].bitcast(I32))
        gt_t = sbuf([P, PACK], F32, "gt_t")
        gp_t = sbuf([P, PACK], F32, "gp_t")
        nc.gpsimd.dma_start(out=gt_t[:], in_=gt.rearrange("(p t) o -> p (t o)", t=PACK))
        nc.gpsimd.dma_start(out=gp_t[:], in_=gp.rearrange("(p t) o -> p (t o)", t=PACK))
        wa_planes = wa.rearrange("(p t) n -> p t n", t=PACK)
        wa_early = sbuf([P, PACK, WA_EARLY[1]], F32, "wa_early")
        nc.sync.dma_start(out=wa_early[:], in_=wa_planes[:, :, 0 : WA_EARLY[1]])

        xs_picked = sbuf([P, D], U8, "xs_picked")
        nc.vector.tensor_copy(out=xs_picked[:], in_=xs_table[:].indirect(offs_t[:]))
        xs_staged = deal(xs_picked, "xs_staged", 1)
        place_scale_rows(x_scale, xs_staged, last_rows)
        wa_late = sbuf([P, PACK, WA_LATE[1]], F32, "wa_late", "xs_picked")
        nc.sync.dma_start(out=wa_late[:], in_=wa_planes[:, :, WA_LATE[0] : D])
        x_codes = sbuf([P, D], U32, "x_codes")
        nc.vector.tensor_copy(out=x_codes[:].rearrange("p (t m) -> p m t", t=PACK), in_=xw_table[:].indirect(offs_t[:]))

        ws_staged = deal(ws_raw, "ws_staged", 1)
        w1_raw = sbuf([P, 2 * D], U8, "w1_raw", "xw_table")
        nc.sync.dma_start(out=w1_raw[:].bitcast(I32), in_=w1_words[0].bitcast(I32))
        w1_scale = w_scales[:, 0:D]
        w2_scale = w_scales[:, D : 2 * D]
        place_scale_rows(w1_scale, ws_staged, w1_rows)
        place_scale_rows(w2_scale, ws_staged, last_rows)
        w2_raw = sbuf([P, 2 * D], U8, "w2_raw", "ws_raw")
        nc.sync.dma_start(out=w2_raw[:].bitcast(I32), in_=w2_words[0].bitcast(I32))
        res_planes = sbuf([P, PACK, D], F32, "res_planes", "wa_early")
        nc.sync.dma_start(out=res_planes[:], in_=res.rearrange("(p t) n -> p t n", t=PACK))

        y_banks = [bank([P, D], "y_bank%d" % t, t) for t in range(PACK)]
        y_late = bank([P, WA_LATE[1]], "y_late", 6)
        wa_woven = [sbuf([P, n, PACK], BF16, "wa_woven%d" % i) for i, (first, n) in enumerate(WA_PIECES)]
        on_scalar = WA_PIECES[0][1]
        dst, src = weave_views(wa_early[:, :, 0:on_scalar], wa_woven[0][:])
        nc.scalar.activation(out=dst, in_=src, func=ACT.Copy)
        weave_on_vector(wa_early[:, :, on_scalar : WA_EARLY[1]], wa_woven[1][:])
        weave_on_vector(wa_late[:], wa_woven[2][:])
        wa_codes = sbuf([P, D], U32, "wa_codes")
        wa_scale = sbuf([P, D], U8, "wa_scale")
        for i, (first, n) in enumerate(WA_PIECES):
            quantize(wa_woven[i][:], wa_codes[:, first : first + n], wa_scale[:, first : first + n])

        def project(t, first, n, out):
            tokens = slice(t * P, (t + 1) * P)
            nc.tensor.matmul_mx(
                out=out,
                lhsT=x_codes[:, tokens].bitcast(FP8X4),
                lhsT_scale=x_scale[:, tokens],
                rhs=wa_codes[:, first : first + n].bitcast(FP8X4),
                rhs_scale=wa_scale[:, first : first + n],
                start=True,
                stop=True,
            )

        y_planes = [sbuf([P, D], F32, "y_plane%d" % t) for t in range(PACK)]
        for first, n in WA_PIECES[:-1]:
            project(0, first, n, y_banks[0][:, first : first + n])
        project(0, WA_LATE[0], WA_LATE[1], y_late[:])
        early = slice(0, WA_EARLY[1])
        nc.scalar.activation(out=y_planes[0][:, early], in_=y_banks[0][:, early], func=ACT.Copy, scale=gt_t[:, 0:1])
        nc.scalar.activation(out=y_planes[0][:, WA_LATE[0] : D], in_=y_late[:], func=ACT.Copy, scale=gt_t[:, 0:1])
        for t in range(1, PACK):
            project(t, 0, D, y_banks[t][:])
        for t in range(1, PACK):
            nc.scalar.activation(out=y_planes[t][:], in_=y_banks[t][:], func=ACT.Copy, scale=gt_t[:, t : t + 1])

        w1_codes = deal(w1_raw, "w1_codes", 2, "wa_woven2")

        def mix(outs, w_codes, w_scale, codes, scale):
            for t in range(PACK):
                nc.tensor.matmul_mx(
                    out=outs[t],
                    lhsT=w_codes[:, 2 * P * t : 2 * P * (t + 1)].bitcast(FP4X4),
                    lhsT_scale=w_scale[:, P * t : P * (t + 1)],
                    rhs=codes.bitcast(FP8X4),
                    rhs_scale=scale,
                    start=True,
                    stop=True,
                )

        half = Z_PIECES[0][1]
        plane_stride = 384
        woven_at = (plane_stride, plane_stride + PACK * half, plane_stride + PACK * half)
        h_planes = [sbuf([P, D], F32, "h_plane%d" % t) for t in range(PACK)]
        z_shared = sbuf([P, woven_at[2] + PACK * Z_PIECES[2][1]], BF16, "z_shared")
        z_codes = sbuf([P, D], U32, "z_codes")
        z_scale = sbuf([P, D], U8, "z_scale")
        first_half = [bank([P, 2, half], "h_first%d" % b, PACK + b) for b in range(2)]
        second_half = [bank([P, half], "h_second%d" % t, t) for t in range(PACK)]
        for i, (first, n) in enumerate(Z_PIECES):
            cols = slice(first, first + n)
            is_last = i == len(Z_PIECES) - 1
            if is_last:
                z_piece = z_shared[:, 0 : PACK * plane_stride].rearrange("p (t n) -> p t n", t=PACK)[:, :, 0:n]
            else:
                z_piece = sbuf([P, PACK, n], BF16, "z_piece%d" % i)[:]
            for t in range(PACK):
                nc.vector.tensor_copy(out=z_piece[:, t, :], in_=y_planes[t][:].indirect(entries(fl_t, first, n)))
            woven = z_shared[:, woven_at[i] : woven_at[i] + PACK * n].rearrange("p (n t) -> p n t", t=PACK)
            if is_last:
                weave_on_vector(z_piece, woven)
            else:
                weave_on_scalar(z_piece, woven)
            quantize(woven, z_codes[:, cols], z_scale[:, cols])
            if first < half:
                outs = [first_half[t // 2][:, t % 2, :] for t in range(PACK)]
            else:
                outs = [second_half[t][:, first - half : first - half + n] for t in range(PACK)]
            mix(outs, w1_codes, w1_scale, z_codes[:, cols], z_scale[:, cols])
            if first < half:
                for t in range(PACK):
                    nc.scalar.activation(out=h_planes[t][:, cols], in_=outs[t], func=ACT.Relu)
        for t in range(PACK):
            nc.scalar.activation(out=h_planes[t][:, half:D], in_=second_half[t][:], func=ACT.Relu)

        w2_codes = deal(w2_raw, "w2_codes", 2, "z_shared")

        z2_codes = sbuf([P, D], U32, "z2_codes")
        z2_scale = sbuf([P, D], U8, "z2_scale")
        out_codes = sbuf([P, D], U32, "out_codes")
        out_scale = sbuf([P, D], U8, "out_scale")
        out_planes = out_0.rearrange("(p t) n -> p t n", t=PACK)
        out_words = out_1[0].rearrange("p n t -> p (n t)").bitcast(I32)
        out_bank_numbers = (6, 7, 4, 5)
        out_banks = []
        h_shared = []
        for i in range(OUT_PIECES):
            first = i * OUT_WIDTH
            cols = slice(first, first + OUT_WIDTH)
            if i < 2:
                h_piece = sbuf([P, PACK, OUT_WIDTH], F32, "h_piece%d" % i)[:]
            else:
                h_piece = h_shared[i - 2][:].rearrange("p (t n) -> p t n", t=PACK)
            z2_piece = sbuf([P, PACK, OUT_WIDTH], BF16, "z2_piece%d" % i)
            for t in range(PACK):
                nc.vector.tensor_copy(out=h_piece[:, t, :], in_=h_planes[t][:].indirect(entries(fm_t, first, OUT_WIDTH)))
                nc.scalar.activation(out=z2_piece[:, t, :], in_=h_piece[:, t, :], func=ACT.Copy, scale=gp_t[:, t : t + 1])
            if i < 2:
                h_shared.append(sbuf([P, PACK * OUT_WIDTH], F32, "h_shared%d" % i))
                woven = h_shared[i][:, OUT_WIDTH : 3 * OUT_WIDTH].bitcast(BF16).rearrange("p (n t) -> p n t", t=PACK)
            else:
                woven = sbuf([P, OUT_WIDTH, PACK], BF16, "z2_woven%d" % i)[:]
            weave_on_scalar(z2_piece[:], woven)
            quantize(woven, z2_codes[:, cols], z2_scale[:, cols])
            acc = bank([P, PACK, OUT_WIDTH], "out_bank%d" % i, out_bank_numbers[i])
            mix([acc[:, t, :] for t in range(PACK)], w2_codes, w2_scale, z2_codes[:, cols], z2_scale[:, cols])
            out_banks.append(acc)

        def finish(i, parts, reuses=None):
            first = i * OUT_WIDTH
            width = OUT_WIDTH // parts
            total = sbuf([P, PACK, OUT_WIDTH], F32, "total%d" % i, reuses)
            total_woven = sbuf([P, OUT_WIDTH, PACK], BF16, "total_woven%d" % i)
            for j in range(parts):
                part = slice(j * width, (j + 1) * width)
                cols = slice(first + j * width, first + (j + 1) * width)
                nc.vector.tensor_tensor(out=total[:, :, part], in0=out_banks[i][:, :, part], in1=res_planes[:, :, cols], op=ALU.add)
            nc.sync.dma_start(out=out_planes[:, :, first : first + OUT_WIDTH], in_=total[:])
            for j in range(parts):
                part = slice(j * width, (j + 1) * width)
                cols = slice(first + j * width, first + (j + 1) * width)
                weave_on_scalar(total[:, :, part], total_woven[:, part, :])
                quantize(total_woven[:, part, :], out_codes[:, cols], out_scale[:, cols])

        def store_words(first_piece, pieces):
            cols = slice(first_piece * OUT_WIDTH, (first_piece + pieces) * OUT_WIDTH)
            nc.sync.dma_start(out=out_words[:, cols], in_=out_codes[:, cols].bitcast(I32))

        finish(1, 1)
        finish(0, 1, "z2_woven2")
        store_words(0, 2)
        finish(2, 1, "z2_woven3")
        store_words(2, 1)
        finish(3, 2)
        store_words(3, 1)
        for q in range(QUADS):
            queue = nc.sync if q % 2 == 0 else nc.scalar
            queue.dma_start(out=out_2[0, 4 * q : 4 * q + 4, :].bitcast(I32), in_=out_scale[32 * q : 32 * q + 4, :].bitcast(I32))
